import numpy as np
import ml_dtypes


def mxq(x, axis, fmt="e4m3"):
    dtype, down = {"e4m3": (ml_dtypes.float8_e4m3fn, 7), "e5m2": (ml_dtypes.float8_e5m2, 14)}[fmt]
    v = np.moveaxis(np.asarray(x, np.float32).astype(ml_dtypes.bfloat16).astype(np.float64), axis, -1)
    blocks = v.reshape(v.shape[:-1] + (-1, 32))
    amax = np.abs(blocks).max(-1, keepdims=True)
    byte = np.maximum(np.where(amax > 0, np.frexp(amax)[1] - 1 + 127, 0) - down, 1)
    scale = np.exp2(byte - 127.0)
    codes = (blocks / scale).astype(np.float32).astype(dtype).astype(np.float64)
    return np.moveaxis((codes * scale).reshape(v.shape), -1, axis)


WIDE = False


def mx_kscale(k):
    if not WIDE:
        return np.ones(k)
    levels = np.array([10, -10, 5, -5, 0])
    if k % 512:
        return np.exp2(np.random.permutation(np.resize(levels, k // 32))).repeat(32)
    a = np.empty((k // 512, 16))
    for p in range(k // 512):
        a[p, :8] = np.random.permutation(np.resize(levels, 8))
        for g in range(8):
            far = levels[np.abs(levels - a[p, g]) >= 10]
            a[p, g + 8] = far[np.random.randint(len(far))]
    return np.exp2(a.ravel()).repeat(32)


def f64(x):
    return np.asarray(x).astype(np.float64)


def striped(idx):
    return np.tile(idx.reshape(-1, 16).T, (8, 1)).astype(np.uint16)


def unstriped(offs):
    return offs[:16].T.reshape(-1).astype(np.int64)


E2M1 = np.array([0.0, 0.5, 1.0, 1.5, 2.0, 3.0, 4.0, 6.0, -0.0, -0.5, -1.0, -1.5, -2.0, -3.0, -4.0, -6.0])


def pack_weight(w, fmt):
    k, n = w.shape
    w = f64(np.asarray(w, np.float32).astype(ml_dtypes.bfloat16)).reshape(k // 32, 32, n)
    amax = np.abs(w).max(1)
    if fmt == "e4m3":
        byte = np.frexp(amax)[1] - 1 + 127 - 7
    else:
        mant, ex = np.frexp(amax / 6.0)
        byte = np.where(mant > 0.5, ex, ex - 1) + 127
    byte = np.clip(np.where(amax > 0, byte, 1), 1, 254)
    scaled = (w * np.exp2(127.0 - byte)[:, None, :]).reshape(k, n).astype(np.float32)
    by_word = np.ascontiguousarray(scaled.reshape(k // 512, 128, 4, n).transpose(0, 1, 3, 2))
    if fmt == "e4m3":
        words = by_word.astype(ml_dtypes.float8_e4m3fn).view(np.uint8)
    else:
        c = by_word.astype(ml_dtypes.float4_e2m1fn).view(np.uint8) & 0xF
        words = (c[..., 0::2] | (c[..., 1::2] << 4)).reshape(k // 512, 128, 2 * n)
    return np.ascontiguousarray(words), np.ascontiguousarray(byte.astype(np.uint8).reshape(k // 512, 16, n))


def unpack_weight(words, scales, fmt):
    g, _, n = scales.shape
    words = np.ascontiguousarray(words).reshape(g, 128, n, -1)
    if fmt == "e4m3":
        vals = words.view(ml_dtypes.float8_e4m3fn).astype(np.float64)
    else:
        nib = np.empty((g, 128, n, 4), np.uint8)
        nib[..., 0::2] = words & 0xF
        nib[..., 1::2] = words >> 4
        vals = E2M1[nib]
    vals = vals * np.repeat(np.exp2(scales.astype(np.float64) - 127.0), 8, axis=1)[..., None]
    return vals.transpose(0, 1, 3, 2).reshape(g * 512, n)


def gelu(v):
    return 0.5 * v * (1.0 + np.tanh(np.sqrt(2.0 / np.pi) * (v + 0.044715 * v**3)))


K, K2, T, T2, S, H, N = 1536, 512, 2048, 2048, 1024, 1024, 512

def setup_inputs():
    n = np.random.standard_normal
    s = mx_kscale(K)[:, None]
    s2 = mx_kscale(K2)[:, None]
    u = mx_kscale(H)[:, None]
    tab_words, tab_scales = pack_weight(n((K, T)) * s, "e4m3")
    tab2_words, tab2_scales = pack_weight(n((K2, T2)) * s2, "e4m3")
    wa_words, wa_scales = pack_weight(n((K, H)) / np.sqrt(K) / s, "e2m1")
    wb = n((K2, H)) / np.sqrt(K2) / s2
    wo = n((H, N)) / np.sqrt(H) / u
    gT = np.exp(0.4 * n((H, T))) * u
    return {
        "tab_words": tab_words, "tab_scales": tab_scales,
        "tab2_words": tab2_words, "tab2_scales": tab2_scales,
        "offs": striped(np.random.permutation(T)[:S]),
        "offs2": striped(np.random.permutation(T2)[:S]),
        "wa_words": wa_words, "wa_scales": wa_scales,
        "wb": wb.astype(np.float32), "wo": wo.astype(np.float32),
        "gT": gT.astype(np.float32), "b": (0.3 * n(N)).astype(np.float32),
    }

def reference(tab_words, tab_scales, tab2_words, tab2_scales, offs, offs2, wa_words, wa_scales, wb, wo, gT, b):
    v = unpack_weight(tab_words, tab_scales, "e4m3")[:, unstriped(offs)]
    v2 = unpack_weight(tab2_words, tab2_scales, "e4m3")[:, unstriped(offs2)]
    g = f64(gT)[:, unstriped(offs)]
    wa = unpack_weight(wa_words, wa_scales, "e2m1")
    p = wa.T @ v
    q = mxq(f64(wb), 0, "e4m3").T @ v2
    h = np.sqrt(np.abs(p * q)) * g
    y = mxq(f64(wo), 0, "e4m3").T @ mxq(h, 0, "e4m3")
    return y + f64(b)[:, None]

@@ -1,0 +1,280 @@
+from contextlib import ExitStack
+
+import concourse.mybir as mybir
+
+K, K2, T, S, H, N = 1536, 512, 2048, 1024, 1024, 512
+FLOPS = 2 * S * (K * H + K2 * H + H * N)
+
+F32 = mybir.dt.float32
+BF16 = mybir.dt.bfloat16
+I32 = mybir.dt.int32
+U32 = mybir.dt.uint32
+U16 = mybir.dt.uint16
+U8 = mybir.dt.uint8
+FP8X4 = mybir.dt.float8_e4m3fn_x4
+FP4X4 = mybir.dt.float4_e2m1fn_x4
+ACT = mybir.ActivationFunctionType
+ALU = mybir.AluOpType
+
+P = 128
+PACK = 4
+KP = P * PACK
+PASSES = K // KP
+BLOCKS = H // KP
+COLS = 512
+HALVES = S // COLS
+LIST_COLS = COLS // 16
+QUADS = 4
+SHIFT_ROWS = 112
+LATE_WORDS = 10 * T + T + PASSES * H // 2 + 64
+
+
+def tile_list_bilinear_region_word_kernel(
+    tc, tab_words, tab_scales, tab2_words, tab2_scales, offs, offs2, wa_words, wa_scales, wb, wo, gT, b, out
+):
+    nc = tc.nc
+    with ExitStack() as ctx:
+        keep = ctx.enter_context(tc.tile_pool(name="keep", bufs=1))
+        results = ctx.enter_context(tc.tile_pool(name="results", bufs=4))
+        psum = ctx.enter_context(tc.psum_pool(name="psum", bufs=4))
+        stage = ctx.enter_context(tc.tile_pool(name="stage", bufs=2))
+
+        list1 = keep.tile([P, S // 16], U16, name="list1")
+        list2 = keep.tile([P, S // 16], U16, name="list2")
+        with tc.tile_pool(name="early", bufs=1) as early:
+            warm = early.tile([P, LATE_WORDS], F32, name="warm")
+            nc.gpsimd.memset(warm[:, 0:1], 1.0)
+            nc.scalar.activation(warm[:, 1:2], warm[:, 0:1], ACT.Sqrt)
+        late = ctx.enter_context(tc.tile_pool(name="late", bufs=1))
+        windows = ctx.enter_context(tc.tile_pool(name="windows", bufs=10))
+
+        def half_of(lst, jh):
+            return lst[:, jh * LIST_COLS : (jh + 1) * LIST_COLS]
+
+        def byte_tile(name, width):
+            return keep.tile([P, width], U8, name=name, align_bytes=64)
+
+        tab2_sc = byte_tile("tab2_sc", T)
+        tab_sc = byte_tile("tab_sc", T)
+        wa_sc_raw = byte_tile("wa_sc_raw", H)
+        v_sc = [byte_tile("v_sc%d" % a, S) for a in range(PASSES)]
+        wa_sc = [byte_tile("wa_sc%d" % a, H) for a in range(PASSES)]
+        v2_sc = byte_tile("v2_sc", S)
+        nc.gpsimd.memset(tab_sc[:].bitcast(I32), 0)
+        for plane in [tab2_sc, wa_sc_raw] + v_sc[1:] + wa_sc[1:]:
+            nc.vector.memset(plane[:].bitcast(I32), 0)
+
+
+        def load_scale_rows(engine, tile, scales):
+            passes = scales.shape[0]
+            for q in range(QUADS):
+                engine.dma_start(
+                    out=tile[32 * q : 32 * q + 4 * passes, :].bitcast(I32),
+                    in_=scales[:, 4 * q : 4 * q + 4, :].bitcast(I32),
+                )
+
+        def load_words(words):
+            w = windows.tile([P, T], I32, name="window", align_bytes=64)
+            nc.sync.dma_start(out=w[:], in_=words.rearrange("p t i -> p (t i)").bitcast(I32))
+            return w
+
+        def load_weight(rows, pool):
+            raw = pool.tile([P, PACK, COLS], F32, name="w_raw")
+            nc.sync.dma_start(out=raw[:], in_=rows.rearrange("(p j) c -> p j c", j=PACK))
+            return raw
+
+        def round_weight(raw):
+            grouped = stage.tile([P, COLS * PACK], BF16, name="w_bf16", align_bytes=64)
+            nc.scalar.copy(
+                out=grouped[:].rearrange("p (t m j) -> p m t j", t=PACK, j=PACK),
+                in_=raw[:].rearrange("p j (m t) -> p m t j", t=PACK),
+            )
+            return grouped
+
+        def quantize(name, grouped):
+            codes = keep.tile([P, COLS], U32, name=name + "_codes", align_bytes=64)
+            scales = byte_tile(name + "_scales", COLS)
+            nc.vector.quantize_mx(out=codes[:].bitcast(FP8X4), scales=scales[:], in_=grouped[:])
+            return codes, scales
+
+        def gather_words(name, window, lst):
+            halves = []
+            for jh in range(HALVES):
+                picked = keep.tile([P, COLS], U32, name="%s_%d" % (name, jh), align_bytes=64)
+                nc.vector.tensor_copy(picked[:], window[:].bitcast(U32).indirect(half_of(lst, jh)))
+                halves.append(picked)
+            return halves
+
+        def shift_planes(planes):
+            for a in range(1, PASSES):
+                nc.gpsimd.dma_start(
+                    out=planes[a][0:SHIFT_ROWS, :].bitcast(I32),
+                    in_=planes[0][4 * a : 4 * a + SHIFT_ROWS, :].bitcast(I32),
+                )
+
+        nc.sync.dma_start(list2[:], offs2)
+        nc.sync.dma_start(list1[:], offs)
+        wb_raw = [load_weight(wb[:, 0:COLS], keep)]
+        load_scale_rows(nc.sync, tab2_sc, tab2_scales)
+        load_scale_rows(nc.gpsimd, tab_sc, tab_scales)
+        tab2_w = load_words(tab2_words[0])
+        load_scale_rows(nc.gpsimd, wa_sc_raw, wa_scales)
+        wb_raw.append(load_weight(wb[:, COLS : 2 * COLS], late))
+        tab_w = [load_words(tab_words[0])]
+        wa_raw = late.tile([P, PASSES, H // 2], I32, name="wa_raw", align_bytes=64)
+        nc.sync.dma_start(out=wa_raw[:], in_=wa_words.rearrange("a p e -> p a e").bitcast(I32))
+        tab_w.extend(load_words(tab_words[a]) for a in range(1, PASSES))
+        g_rows = gT.rearrange("(blk p t) c -> blk t p c", p=P, t=PACK)
+        gates = {}
+        wo_raw = []
+        for blk in range(BLOCKS):
+            for t in range(PACK):
+                g = windows.tile([P, T], F32, name="window", align_bytes=64)
+                nc.sync.dma_start(out=g[:], in_=g_rows[blk, t])
+                gates[blk, t] = g
+            wo_raw.append(load_weight(wo[blk * KP : (blk + 1) * KP, :], (keep, late)[blk]))
+        bias = late.tile([P, PACK], F32, name="bias")
+        nc.sync.dma_start(out=bias[:], in_=b.rearrange("(p c) -> p c", c=PACK))
+
+        nc.vector.tensor_copy(v2_sc[:], tab2_sc[:].indirect(list2[:]))
+        wb_bf = [round_weight(raw) for raw in wb_raw]
+        v2 = gather_words("v2", tab2_w, list2)
+        wbq = [quantize("wb0", wb_bf[0])]
+        nc.vector.tensor_copy(v_sc[0][:], tab_sc[:].indirect(list1[:]))
+        shift_planes(v_sc)
+        nc.vector.tensor_copy(
+            out=wa_sc[0][:].rearrange("p (blk t m) -> p blk t m", blk=BLOCKS, t=PACK),
+            in_=wa_sc_raw[:].rearrange("p (blk m t) -> p blk t m", blk=BLOCKS, t=PACK),
+        )
+        shift_planes(wa_sc)
+        v = [gather_words("v0", tab_w[0], list1)]
+        wbq.append(quantize("wb1", wb_bf[1]))
+
+        units = [(blk, jh, t) for blk in range(BLOCKS) for jh in range(HALVES) for t in range(PACK)]
+        work = {}
+        for blk, jh, t in units:
+            acc = psum.tile([P, COLS], F32, name="acc")
+            codes, scales = wbq[blk]
+            nc.tensor.matmul_mx(
+                out=acc[:],
+                lhsT=codes[:, t * P : (t + 1) * P].bitcast(FP8X4),
+                lhsT_scale=scales[:, t * P : (t + 1) * P],
+                rhs=v2[jh][:].bitcast(FP8X4),
+                rhs_scale=v2_sc[:, jh * COLS : (jh + 1) * COLS],
+                start=True,
+                stop=True,
+            )
+            w = keep.tile([P, COLS], F32, name="work_%d_%d_%d" % (blk, jh, t))
+            nc.scalar.activation(w[:], acc[:], ACT.Copy)
+            work[blk, jh, t] = w
+
+        wa_dealt = []
+        for blk in range(BLOCKS):
+            dealt = keep.tile([P, PASSES, 2 * KP], U8, name="wa_dealt%d" % blk, align_bytes=64)
+            nc.vector.tensor_copy(
+                out=dealt[:].bitcast(U16).rearrange("p a (t m) -> p a t m", t=PACK),
+                in_=wa_raw[:].bitcast(U16)[:, :, blk * KP : (blk + 1) * KP].rearrange("p a (m t) -> p a t m", t=PACK),
+            )
+            wa_dealt.append(dealt)
+        v.extend(gather_words("v%d" % a, tab_w[a], list1) for a in range(1, PASSES))
+
+
+        def project(unit):
+            blk, jh, t = unit
+            acc = psum.tile([P, COLS], F32, name="acc")
+            col = blk * KP + t * P
+            for a in range(PASSES):
+                nc.tensor.matmul_mx(
+                    out=acc[:],
+                    lhsT=wa_dealt[blk][:, a, 2 * t * P : 2 * (t + 1) * P].bitcast(FP4X4),
+                    lhsT_scale=wa_sc[a][:, col : col + P],
+                    rhs=v[a][jh][:].bitcast(FP8X4),
+                    rhs_scale=v_sc[a][:, jh * COLS : (jh + 1) * COLS],
+                    start=(a == 0),
+                    stop=(a == PASSES - 1),
+                )
+            w = work[unit]
+            nc.vector.tensor_tensor(w[:], acc[:], w[:], ALU.mult)
+            nc.scalar.activation(w[:], w[:], ACT.Abs)
+            nc.scalar.activation(w[:], w[:], ACT.Sqrt)
+
+        pooled = {}
+
+        def gate(unit):
+            blk, jh, t = unit
+            if t == 0:
+                pooled[blk, jh] = stage.tile([P, PACK, COLS], F32, name="pooled")
+            nc.vector.tensor_tensor(
+                pooled[blk, jh][:, t, :], gates[blk, t][:].indirect(half_of(list1, jh)), work[unit][:], ALU.mult
+            )
+
+        rounded = {}
+
+        def round_pooled(group, on_vector):
+            r = stage.tile([P, COLS * PACK], BF16, name="pooled_bf16", align_bytes=64)
+            dst = r[:].rearrange("p (c i t) -> p c t i", i=4, t=PACK)
+            src = pooled[group][:].rearrange("p t (c i) -> p c t i", i=4)
+            if on_vector:
+                nc.vector.tensor_copy(out=dst, in_=src)
+            else:
+                nc.scalar.copy(out=dst, in_=src)
+            rounded[group] = r
+
+        hq = {}
+        woq = []
+        banks = {}
+        out_rows = out.rearrange("(p c) j -> c p j", c=PACK)
+
+        def fuse_pass(jh, blk):
+            for c in range(PACK):
+                if blk == 0:
+                    banks[jh, c] = psum.tile([P, COLS], F32, name="fused")
+                nc.tensor.matmul_mx(
+                    out=banks[jh, c][:],
+                    lhsT=woq[blk][0][:, c * P : (c + 1) * P].bitcast(FP8X4),
+                    lhsT_scale=woq[blk][1][:, c * P : (c + 1) * P],
+                    rhs=hq[blk, jh][0][:].bitcast(FP8X4),
+                    rhs_scale=hq[blk, jh][1][:],
+                    start=(blk == 0),
+                    stop=(blk == BLOCKS - 1),
+                )
+
+        def store(jh, share_with_vector):
+            for c in range(PACK):
+                y = results.tile([P, COLS], F32, name="y")
+                if share_with_vector and c % 2 == 1:
+                    nc.vector.tensor_scalar(y[:], banks[jh, c][:], bias[:, c : c + 1], None, ALU.add)
+                else:
+                    nc.scalar.activation(y[:], banks[jh, c][:], ACT.Identity, bias=bias[:, c : c + 1])
+                nc.sync.dma_start(out=out_rows[c][:, jh * COLS : (jh + 1) * COLS], in_=y[:])
+
+        LAG = 2
+        for u in range(len(units) + LAG):
+            if u < len(units):
+                project(units[u])
+            if u >= LAG:
+                gate(units[u - LAG])
+            if u == 7:
+                round_pooled((0, 0), False)
+            if u == 9:
+                hq[0, 0] = quantize("h00", rounded[0, 0])
+                wo_bf0 = round_weight(wo_raw[0])
+            if u == 11:
+                woq.append(quantize("wo0", wo_bf0))
+                round_pooled((0, 1), False)
+            if u == 13:
+                hq[0, 1] = quantize("h01", rounded[0, 1])
+                wo_bf1 = round_weight(wo_raw[1])
+            if u == 15:
+                woq.append(quantize("wo1", wo_bf1))
+                fuse_pass(0, 0)
+                round_pooled((1, 0), False)
+            if u == 16:
+                hq[1, 0] = quantize("h10", rounded[1, 0])
+                fuse_pass(0, 1)
+                store(0, False)
+        fuse_pass(1, 0)
+        round_pooled((1, 1), True)
+        hq[1, 1] = quantize("h11", rounded[1, 1])
+        fuse_pass(1, 1)
+        store(1, True)

@@ -26,7 +26,6 @@ HALVES = S // COLS
 LIST_COLS = COLS // 16
 QUADS = 4
 SHIFT_ROWS = 112
-LATE_WORDS = 10 * T + T + PASSES * H // 2 + 64
 
 
 def tile_list_bilinear_region_word_kernel(
@@ -35,18 +34,13 @@ def tile_list_bilinear_region_word_kernel(
     nc = tc.nc
     with ExitStack() as ctx:
         keep = ctx.enter_context(tc.tile_pool(name="keep", bufs=1))
-        results = ctx.enter_context(tc.tile_pool(name="results", bufs=4))
-        psum = ctx.enter_context(tc.psum_pool(name="psum", bufs=4))
+        windows = ctx.enter_context(tc.tile_pool(name="windows", bufs=9))
         stage = ctx.enter_context(tc.tile_pool(name="stage", bufs=2))
+        results = ctx.enter_context(tc.tile_pool(name="results", bufs=1))
+        psum = ctx.enter_context(tc.psum_pool(name="psum", bufs=4))
 
         list1 = keep.tile([P, S // 16], U16, name="list1")
         list2 = keep.tile([P, S // 16], U16, name="list2")
-        with tc.tile_pool(name="early", bufs=1) as early:
-            warm = early.tile([P, LATE_WORDS], F32, name="warm")
-            nc.gpsimd.memset(warm[:, 0:1], 1.0)
-            nc.scalar.activation(warm[:, 1:2], warm[:, 0:1], ACT.Sqrt)
-        late = ctx.enter_context(tc.tile_pool(name="late", bufs=1))
-        windows = ctx.enter_context(tc.tile_pool(name="windows", bufs=10))
 
         def half_of(lst, jh):
             return lst[:, jh * LIST_COLS : (jh + 1) * LIST_COLS]
@@ -60,10 +54,13 @@ def tile_list_bilinear_region_word_kernel(
         v_sc = [byte_tile("v_sc%d" % a, S) for a in range(PASSES)]
         wa_sc = [byte_tile("wa_sc%d" % a, H) for a in range(PASSES)]
         v2_sc = byte_tile("v2_sc", S)
-        nc.gpsimd.memset(tab_sc[:].bitcast(I32), 0)
-        for plane in [tab2_sc, wa_sc_raw] + v_sc[1:] + wa_sc[1:]:
+        nc.gpsimd.memset(tab2_sc[:].bitcast(I32), 0)
+        for plane in [tab_sc, wa_sc_raw] + v_sc[1:] + wa_sc[1:]:
             nc.vector.memset(plane[:].bitcast(I32), 0)
 
+        warm = keep.tile([P, 2], F32, name="warm")
+        nc.vector.memset(warm[:, 0:1], 1.0)
+        nc.scalar.activation(warm[:, 1:2], warm[:, 0:1], ACT.Sqrt)
 
         def load_scale_rows(engine, tile, scales):
             passes = scales.shape[0]
@@ -73,13 +70,13 @@ def tile_list_bilinear_region_word_kernel(
                     in_=scales[:, 4 * q : 4 * q + 4, :].bitcast(I32),
                 )
 
-        def load_words(words):
-            w = windows.tile([P, T], I32, name="window", align_bytes=64)
+        def load_words(words, pool=windows, tag="window"):
+            w = pool.tile([P, T], I32, name=tag, align_bytes=64)
             nc.sync.dma_start(out=w[:], in_=words.rearrange("p t i -> p (t i)").bitcast(I32))
             return w
 
-        def load_weight(rows, pool):
-            raw = pool.tile([P, PACK, COLS], F32, name="w_raw")
+        def load_weight(rows, pool=stage, tag="w_raw"):
+            raw = pool.tile([P, PACK, COLS], F32, name=tag)
             nc.sync.dma_start(out=raw[:], in_=rows.rearrange("(p j) c -> p j c", j=PACK))
             return raw
 
@@ -91,9 +88,10 @@ def tile_list_bilinear_region_word_kernel(
             )
             return grouped
 
-        def quantize(name, grouped):
-            codes = keep.tile([P, COLS], U32, name=name + "_codes", align_bytes=64)
-            scales = byte_tile(name + "_scales", COLS)
+        def quantize(name, grouped, tag=None):
+            width = grouped.shape[1] // PACK
+            codes = keep.tile([P, width], U32, name=tag or name + "_codes", align_bytes=64)
+            scales = byte_tile(name + "_scales", width)
             nc.vector.quantize_mx(out=codes[:].bitcast(FP8X4), scales=scales[:], in_=grouped[:])
             return codes, scales
 
@@ -107,52 +105,77 @@ def tile_list_bilinear_region_word_kernel(
 
         def shift_planes(planes):
             for a in range(1, PASSES):
-                nc.gpsimd.dma_start(
+                nc.sync.dma_start(
                     out=planes[a][0:SHIFT_ROWS, :].bitcast(I32),
                     in_=planes[0][4 * a : 4 * a + SHIFT_ROWS, :].bitcast(I32),
                 )
 
+        wb_raw, wb_bf, wbq, tab_w, v, wo_raw, gates, wa_dealt = {}, {}, {}, {}, {}, {}, {}, {}
+        wa_raw = keep.tile([P, PASSES, H // 2], I32, name="wa_raw", align_bytes=64)
+        bias = keep.tile([P, PACK], F32, name="bias")
+        g_rows = gT.rearrange("(blk p t) c -> blk t p c", p=P, t=PACK)
+
+        def load_gate(blk, t):
+            g = windows.tile([P, T], F32, name="window", align_bytes=64)
+            nc.sync.dma_start(out=g[:], in_=g_rows[blk, t])
+            gates[blk, t] = g
+
+        def deal(blk):
+            dealt = keep.tile([P, PASSES, 2 * KP], U8, name="wa_dealt%d" % blk, align_bytes=64)
+            nc.vector.tensor_copy(
+                out=dealt[:].bitcast(U16).rearrange("p a (t m) -> p a t m", t=PACK),
+                in_=wa_raw[:].bitcast(U16)[:, :, blk * KP : (blk + 1) * KP].rearrange("p a (m t) -> p a t m", t=PACK),
+            )
+            wa_dealt[blk] = dealt
+
         nc.sync.dma_start(list2[:], offs2)
         nc.sync.dma_start(list1[:], offs)
-        wb_raw = [load_weight(wb[:, 0:COLS], keep)]
+        wb_raw[0] = load_weight(wb[:, 0:COLS], keep, "slot0")
         load_scale_rows(nc.sync, tab2_sc, tab2_scales)
-        load_scale_rows(nc.gpsimd, tab_sc, tab_scales)
         tab2_w = load_words(tab2_words[0])
-        load_scale_rows(nc.gpsimd, wa_sc_raw, wa_scales)
-        wb_raw.append(load_weight(wb[:, COLS : 2 * COLS], late))
-        tab_w = [load_words(tab_words[0])]
-        wa_raw = late.tile([P, PASSES, H // 2], I32, name="wa_raw", align_bytes=64)
+        load_scale_rows(nc.sync, tab_sc, tab_scales)
+        wb_raw[1] = load_weight(wb[:, COLS : 2 * COLS], keep, "slot1")
+        tab_w[0] = load_words(tab_words[0])
+        load_scale_rows(nc.sync, wa_sc_raw, wa_scales)
         nc.sync.dma_start(out=wa_raw[:], in_=wa_words.rearrange("a p e -> p a e").bitcast(I32))
-        tab_w.extend(load_words(tab_words[a]) for a in range(1, PASSES))
-        g_rows = gT.rearrange("(blk p t) c -> blk t p c", p=P, t=PACK)
-        gates = {}
-        wo_raw = []
-        for blk in range(BLOCKS):
-            for t in range(PACK):
-                g = windows.tile([P, T], F32, name="window", align_bytes=64)
-                nc.sync.dma_start(out=g[:], in_=g_rows[blk, t])
-                gates[blk, t] = g
-            wo_raw.append(load_weight(wo[blk * KP : (blk + 1) * KP, :], (keep, late)[blk]))
-        bias = late.tile([P, PACK], F32, name="bias")
-        nc.sync.dma_start(out=bias[:], in_=b.rearrange("(p c) -> p c", c=PACK))
-
+        tab_w[1] = load_words(tab_words[1])
         nc.vector.tensor_copy(v2_sc[:], tab2_sc[:].indirect(list2[:]))
-        wb_bf = [round_weight(raw) for raw in wb_raw]
-        v2 = gather_words("v2", tab2_w, list2)
-        wbq = [quantize("wb0", wb_bf[0])]
+        v2 = gather_words("words", tab2_w, list2)
+        wb_bf[0] = round_weight(wb_raw[0])
+        wb_bf[1] = round_weight(wb_raw[1])
+        wbq[0] = quantize("wb0", wb_bf[0], "tab2_sc")
         nc.vector.tensor_copy(v_sc[0][:], tab_sc[:].indirect(list1[:]))
         shift_planes(v_sc)
+        tab_w[2] = load_words(tab_words[2], keep, "wa_dealt1")
+        v[0] = gather_words("v0", tab_w[0], list1)
         nc.vector.tensor_copy(
             out=wa_sc[0][:].rearrange("p (blk t m) -> p blk t m", blk=BLOCKS, t=PACK),
             in_=wa_sc_raw[:].rearrange("p (blk m t) -> p blk t m", blk=BLOCKS, t=PACK),
         )
         shift_planes(wa_sc)
-        v = [gather_words("v0", tab_w[0], list1)]
-        wbq.append(quantize("wb1", wb_bf[1]))
+        wbq[1] = quantize("wb1", wb_bf[1], "wa_sc_raw")
+        deal(0)
+        v[1] = gather_words("v1", tab_w[1], list1)
+        v[2] = gather_words("v2", tab_w[2], list1)
+        deal(1)
+        load_gate(0, 0)
+        load_gate(0, 1)
+        load_gate(0, 2)
+        load_gate(0, 3)
+        wo_raw[0] = load_weight(wo[0:KP, :])
+        wo_raw[1] = load_weight(wo[KP : 2 * KP, :])
+        nc.sync.dma_start(out=bias[:], in_=b.rearrange("(p c) -> p c", c=PACK))
+        load_gate(1, 0)
+        load_gate(1, 1)
+        load_gate(1, 2)
+        load_gate(1, 3)
 
         units = [(blk, jh, t) for blk in range(BLOCKS) for jh in range(HALVES) for t in range(PACK)]
+        groups = [(blk, jh) for blk in range(BLOCKS) for jh in range(HALVES)]
         work = {}
         for blk, jh, t in units:
+            if t == 0:
+                work[blk, jh] = keep.tile([P, PACK, COLS], F32, name="slot%d" % (groups.index((blk, jh)) + 1))
             acc = psum.tile([P, COLS], F32, name="acc")
             codes, scales = wbq[blk]
             nc.tensor.matmul_mx(
@@ -164,24 +187,11 @@ def tile_list_bilinear_region_word_kernel(
                 start=True,
                 stop=True,
             )
-            w = keep.tile([P, COLS], F32, name="work_%d_%d_%d" % (blk, jh, t))
-            nc.scalar.activation(w[:], acc[:], ACT.Copy)
-            work[blk, jh, t] = w
-
-        wa_dealt = []
-        for blk in range(BLOCKS):
-            dealt = keep.tile([P, PASSES, 2 * KP], U8, name="wa_dealt%d" % blk, align_bytes=64)
-            nc.vector.tensor_copy(
-                out=dealt[:].bitcast(U16).rearrange("p a (t m) -> p a t m", t=PACK),
-                in_=wa_raw[:].bitcast(U16)[:, :, blk * KP : (blk + 1) * KP].rearrange("p a (m t) -> p a t m", t=PACK),
-            )
-            wa_dealt.append(dealt)
-        v.extend(gather_words("v%d" % a, tab_w[a], list1) for a in range(1, PASSES))
-
+            nc.scalar.activation(work[blk, jh][:, t, :], acc[:], ACT.Copy)
 
         def project(unit):
             blk, jh, t = unit
-            acc = psum.tile([P, COLS], F32, name="acc")
+            acc = psum.tile([P, COLS], F32, name="fused")
             col = blk * KP + t * P
             for a in range(PASSES):
                 nc.tensor.matmul_mx(
@@ -193,88 +203,117 @@ def tile_list_bilinear_region_word_kernel(
                     start=(a == 0),
                     stop=(a == PASSES - 1),
                 )
-            w = work[unit]
-            nc.vector.tensor_tensor(w[:], acc[:], w[:], ALU.mult)
-            nc.scalar.activation(w[:], w[:], ACT.Abs)
-            nc.scalar.activation(w[:], w[:], ACT.Sqrt)
+            w = work[blk, jh][:, t, :]
+            nc.vector.tensor_tensor(w, acc[:], w, ALU.mult)
+            nc.scalar.activation(w, w, ACT.Abs)
+            nc.scalar.activation(w, w, ACT.Sqrt)
 
         pooled = {}
 
-        def gate(unit):
-            blk, jh, t = unit
-            if t == 0:
-                pooled[blk, jh] = stage.tile([P, PACK, COLS], F32, name="pooled")
-            nc.vector.tensor_tensor(
-                pooled[blk, jh][:, t, :], gates[blk, t][:].indirect(half_of(list1, jh)), work[unit][:], ALU.mult
+        def gate(group, c0, c1, slots=range(PACK)):
+            blk, jh = group
+            if group not in pooled:
+                pooled[group] = keep.tile([P, PACK, COLS], F32, name="slot%d" % groups.index(group))
+            first = (jh * COLS + c0) // 16
+            offsets = list1[:, first : first + (c1 - c0) // 16]
+            for t in slots:
+                nc.vector.tensor_tensor(
+                    pooled[group][:, t, c0:c1], gates[blk, t][:].indirect(offsets), work[group][:, t, c0:c1], ALU.mult
+                )
+
+        def round_pooled(group, c0, c1, copy):
+            r = stage.tile([P, (c1 - c0) * PACK], BF16, name="pooled_bf16", align_bytes=64, bufs=3)
+            copy(
+                out=r[:].rearrange("p (c i t) -> p c t i", i=4, t=PACK),
+                in_=pooled[group][:, :, c0:c1].rearrange("p t (c i) -> p c t i", i=4),
             )
+            return r
 
-        rounded = {}
+        out_rows = out.rearrange("(p c) j -> p c j", c=PACK)
 
-        def round_pooled(group, on_vector):
-            r = stage.tile([P, COLS * PACK], BF16, name="pooled_bf16", align_bytes=64)
-            dst = r[:].rearrange("p (c i t) -> p c t i", i=4, t=PACK)
-            src = pooled[group][:].rearrange("p t (c i) -> p c t i", i=4)
-            if on_vector:
-                nc.vector.tensor_copy(out=dst, in_=src)
-            else:
-                nc.scalar.copy(out=dst, in_=src)
-            rounded[group] = r
-
-        hq = {}
-        woq = []
-        banks = {}
-        out_rows = out.rearrange("(p c) j -> c p j", c=PACK)
-
-        def fuse_pass(jh, blk):
+        def fuse_pass(banks, blk, hq, c0, c1):
+            codes, scales = hq
             for c in range(PACK):
-                if blk == 0:
-                    banks[jh, c] = psum.tile([P, COLS], F32, name="fused")
                 nc.tensor.matmul_mx(
-                    out=banks[jh, c][:],
+                    out=banks[c][:, 0 : c1 - c0],
                     lhsT=woq[blk][0][:, c * P : (c + 1) * P].bitcast(FP8X4),
                     lhsT_scale=woq[blk][1][:, c * P : (c + 1) * P],
-                    rhs=hq[blk, jh][0][:].bitcast(FP8X4),
-                    rhs_scale=hq[blk, jh][1][:],
+                    rhs=codes[:, c0:c1].bitcast(FP8X4),
+                    rhs_scale=scales[:, c0:c1],
                     start=(blk == 0),
                     stop=(blk == BLOCKS - 1),
                 )
 
-        def store(jh, share_with_vector):
-            for c in range(PACK):
-                y = results.tile([P, COLS], F32, name="y")
-                if share_with_vector and c % 2 == 1:
-                    nc.vector.tensor_scalar(y[:], banks[jh, c][:], bias[:, c : c + 1], None, ALU.add)
-                else:
-                    nc.scalar.activation(y[:], banks[jh, c][:], ACT.Identity, bias=bias[:, c : c + 1])
-                nc.sync.dma_start(out=out_rows[c][:, jh * COLS : (jh + 1) * COLS], in_=y[:])
+        def store(banks, j0, width, share_with_vector):
+            for pair in range(PACK // 2):
+                y = results.tile([P, 2, width], F32, name="y_%d_%d" % (j0, pair))
+                for i in range(2):
+                    c = 2 * pair + i
+                    if share_with_vector and pair == 1:
+                        nc.vector.tensor_scalar(y[:, i, :], banks[c][:, 0:width], bias[:, c : c + 1], None, ALU.add)
+                    else:
+                        nc.scalar.activation(y[:, i, :], banks[c][:, 0:width], ACT.Identity, bias=bias[:, c : c + 1])
+                nc.sync.dma_start(out=out_rows[:, 2 * pair : 2 * pair + 2, j0 : j0 + width], in_=y[:])
 
-        LAG = 2
-        for u in range(len(units) + LAG):
-            if u < len(units):
-                project(units[u])
-            if u >= LAG:
-                gate(units[u - LAG])
-            if u == 7:
-                round_pooled((0, 0), False)
-            if u == 9:
-                hq[0, 0] = quantize("h00", rounded[0, 0])
-                wo_bf0 = round_weight(wo_raw[0])
-            if u == 11:
-                woq.append(quantize("wo0", wo_bf0))
-                round_pooled((0, 1), False)
-            if u == 13:
-                hq[0, 1] = quantize("h01", rounded[0, 1])
-                wo_bf1 = round_weight(wo_raw[1])
-            if u == 15:
-                woq.append(quantize("wo1", wo_bf1))
-                fuse_pass(0, 0)
-                round_pooled((1, 0), False)
-            if u == 16:
-                hq[1, 0] = quantize("h10", rounded[1, 0])
-                fuse_pass(0, 1)
-                store(0, False)
-        fuse_pass(1, 0)
-        round_pooled((1, 1), True)
-        hq[1, 1] = quantize("h11", rounded[1, 1])
-        fuse_pass(1, 1)
-        store(1, True)
+        def open_banks(tag):
+            return [psum.tile([P, COLS], F32, name=tag) for c in range(PACK)]
+
+        half = COLS // 2
+        last = groups[-1]
+        woq, wo_bf, hq, h_bf = {}, {}, {}, {}
+        project(units[0])
+        project(units[1])
+        project(units[2])
+        gate(units[0][:2], 0, COLS, [units[0][2]])
+        project(units[3])
+        gate(units[1][:2], 0, COLS, [units[1][2]])
+        project(units[4])
+        gate(units[2][:2], 0, COLS, [units[2][2]])
+        project(units[5])
+        gate(units[3][:2], 0, COLS, [units[3][2]])
+        project(units[6])
+        gate(units[4][:2], 0, COLS, [units[4][2]])
+        project(units[7])
+        gate(units[5][:2], 0, COLS, [units[5][2]])
+        wo_bf[0] = round_weight(wo_raw[0])
+        project(units[8])
+        gate(units[6][:2], 0, COLS, [units[6][2]])
+        project(units[9])
+        gate(units[7][:2], 0, COLS, [units[7][2]])
+        woq[0] = quantize("wo0", wo_bf[0])
+        h_bf[0, 0] = round_pooled((0, 0), 0, COLS, nc.scalar.copy)
+        project(units[10])
+        gate(units[8][:2], 0, COLS, [units[8][2]])
+        project(units[11])
+        gate(units[9][:2], 0, COLS, [units[9][2]])
+        hq[0, 0] = quantize("h00", h_bf[0, 0])
+        wo_bf[1] = round_weight(wo_raw[1])
+        project(units[12])
+        gate(units[10][:2], 0, COLS, [units[10][2]])
+        project(units[13])
+        woq[1] = quantize("wo1", wo_bf[1])
+        project(units[14])
+        project(units[15])
+        gate(units[11][:2], 0, COLS, [units[11][2]])
+        h_bf[1, 0] = round_pooled((1, 0), 0, COLS, nc.vector.tensor_copy)
+        h_bf[0, 1] = round_pooled((0, 1), 0, COLS, nc.scalar.copy)
+        banks_0 = open_banks("acc")
+        fuse_pass(banks_0, 0, hq[0, 0], 0, COLS)
+        gate(last, 0, half)
+        hq[1, 0] = quantize("h10", h_bf[1, 0])
+        hq[0, 1] = quantize("h01", h_bf[0, 1])
+        fuse_pass(banks_0, 1, hq[1, 0], 0, COLS)
+        banks_a = open_banks("fused")
+        fuse_pass(banks_a, 0, hq[0, 1], 0, half)
+        h_a = round_pooled(last, 0, half, nc.scalar.copy)
+        store(banks_0, 0, COLS, False)
+        hq_a = quantize("h11a", h_a)
+        banks_b = open_banks("acc")
+        fuse_pass(banks_b, 0, hq[0, 1], half, COLS)
+        gate(last, half, COLS)
+        fuse_pass(banks_a, 1, hq_a, 0, half)
+        store(banks_a, COLS, half, False)
+        h_b = round_pooled(last, half, COLS, nc.vector.tensor_copy)
+        hq_b = quantize("h11b", h_b)
+        fuse_pass(banks_b, 1, hq_b, 0, half)
+        store(banks_b, COLS + half, half, True)

@@ -34,7 +34,7 @@ def tile_list_bilinear_region_word_kernel(
     nc = tc.nc
     with ExitStack() as ctx:
         keep = ctx.enter_context(tc.tile_pool(name="keep", bufs=1))
-        windows = ctx.enter_context(tc.tile_pool(name="windows", bufs=9))
+        windows = ctx.enter_context(tc.tile_pool(name="windows", bufs=10))
         stage = ctx.enter_context(tc.tile_pool(name="stage", bufs=2))
         results = ctx.enter_context(tc.tile_pool(name="results", bufs=1))
         psum = ctx.enter_context(tc.psum_pool(name="psum", bufs=4))
@@ -83,8 +83,16 @@ def tile_list_bilinear_region_word_kernel(
         def round_weight(raw):
             grouped = stage.tile([P, COLS * PACK], BF16, name="w_bf16", align_bytes=64)
             nc.scalar.copy(
-                out=grouped[:].rearrange("p (t m j) -> p m t j", t=PACK, j=PACK),
-                in_=raw[:].rearrange("p j (m t) -> p m t j", t=PACK),
+                out=grouped[:].rearrange("p (t m j) -> p m j t", t=PACK, j=PACK),
+                in_=raw[:].rearrange("p j (m t) -> p m j t", t=PACK),
+            )
+            return grouped
+
+        def round_wo(raw):
+            grouped = stage.tile([P, COLS * PACK], BF16, name="w_bf16", align_bytes=64)
+            nc.scalar.copy(
+                out=grouped[:].rearrange("p (c i j) -> p c j i", i=4, j=PACK),
+                in_=raw[:].rearrange("p j (c i) -> p c j i", i=4),
             )
             return grouped
 
@@ -128,10 +136,11 @@ def tile_list_bilinear_region_word_kernel(
             )
             wa_dealt[blk] = dealt
 
+        wb_raw[0] = load_weight(wb[:, 0:COLS], keep, "slot0")
         nc.sync.dma_start(list2[:], offs2)
         nc.sync.dma_start(list1[:], offs)
-        wb_raw[0] = load_weight(wb[:, 0:COLS], keep, "slot0")
-        load_scale_rows(nc.sync, tab2_sc, tab2_scales)
+        for r in range(4):
+            nc.sync.dma_start(out=tab2_sc[r:P:32, :].bitcast(I32), in_=tab2_scales[0, r:16:4, :].bitcast(I32))
         tab2_w = load_words(tab2_words[0])
         load_scale_rows(nc.sync, tab_sc, tab_scales)
         wb_raw[1] = load_weight(wb[:, COLS : 2 * COLS], keep, "slot1")
@@ -145,8 +154,8 @@ def tile_list_bilinear_region_word_kernel(
         wb_bf[1] = round_weight(wb_raw[1])
         wbq[0] = quantize("wb0", wb_bf[0], "tab2_sc")
         nc.vector.tensor_copy(v_sc[0][:], tab_sc[:].indirect(list1[:]))
+        tab_w[2] = load_words(tab_words[2])
         shift_planes(v_sc)
-        tab_w[2] = load_words(tab_words[2], keep, "wa_dealt1")
         v[0] = gather_words("v0", tab_w[0], list1)
         nc.vector.tensor_copy(
             out=wa_sc[0][:].rearrange("p (blk t m) -> p blk t m", blk=BLOCKS, t=PACK),
@@ -164,7 +173,8 @@ def tile_list_bilinear_region_word_kernel(
         load_gate(0, 3)
         wo_raw[0] = load_weight(wo[0:KP, :])
         wo_raw[1] = load_weight(wo[KP : 2 * KP, :])
-        nc.sync.dma_start(out=bias[:], in_=b.rearrange("(p c) -> p c", c=PACK))
+        with nc.allow_non_contiguous_dma(reason="one bias value a partition and output tile"):
+            nc.sync.dma_start(out=bias[:], in_=b.rearrange("(c p) -> p c", p=P))
         load_gate(1, 0)
         load_gate(1, 1)
         load_gate(1, 2)
@@ -229,7 +239,7 @@ def tile_list_bilinear_region_word_kernel(
             )
             return r
 
-        out_rows = out.rearrange("(p c) j -> p c j", c=PACK)
+        out_rows = out.rearrange("(c p) j -> p c j", p=P)
 
         def fuse_pass(banks, blk, hq, c0, c1):
             codes, scales = hq
@@ -275,7 +285,7 @@ def tile_list_bilinear_region_word_kernel(
         gate(units[4][:2], 0, COLS, [units[4][2]])
         project(units[7])
         gate(units[5][:2], 0, COLS, [units[5][2]])
-        wo_bf[0] = round_weight(wo_raw[0])
+        wo_bf[0] = round_wo(wo_raw[0])
         project(units[8])
         gate(units[6][:2], 0, COLS, [units[6][2]])
         project(units[9])
@@ -287,7 +297,7 @@ def tile_list_bilinear_region_word_kernel(
         project(units[11])
         gate(units[9][:2], 0, COLS, [units[9][2]])
         hq[0, 0] = quantize("h00", h_bf[0, 0])
-        wo_bf[1] = round_weight(wo_raw[1])
+        wo_bf[1] = round_wo(wo_raw[1])
         project(units[12])
         gate(units[10][:2], 0, COLS, [units[10][2]])
         project(units[13])

@@ -21,11 +21,15 @@ PACK = 4
 KP = P * PACK
 PASSES = K // KP
 BLOCKS = H // KP
-COLS = 512
-HALVES = S // COLS
-LIST_COLS = COLS // 16
-QUADS = 4
+BANK = 512
+QUARTER = S // 4
+PER_COLUMN = 16
+QUADRANTS = 4
+ROWS = 4
 SHIFT_ROWS = 112
+LAG = 2
+FIRST_ROUND = 7
+NEIGHBOURS = 4
 
 
 def tile_list_bilinear_region_word_kernel(
@@ -35,217 +39,183 @@ def tile_list_bilinear_region_word_kernel(
     with ExitStack() as ctx:
         keep = ctx.enter_context(tc.tile_pool(name="keep", bufs=1))
         windows = ctx.enter_context(tc.tile_pool(name="windows", bufs=10))
-        stage = ctx.enter_context(tc.tile_pool(name="stage", bufs=2))
-        results = ctx.enter_context(tc.tile_pool(name="results", bufs=1))
+        stage = ctx.enter_context(tc.tile_pool(name="stage", bufs=3))
         psum = ctx.enter_context(tc.psum_pool(name="psum", bufs=4))
 
-        list1 = keep.tile([P, S // 16], U16, name="list1")
-        list2 = keep.tile([P, S // 16], U16, name="list2")
+        list1 = keep.tile([P, S // PER_COLUMN], U16, name="list1")
+        list2 = keep.tile([P, S // PER_COLUMN], U16, name="list2")
 
-        def half_of(lst, jh):
-            return lst[:, jh * LIST_COLS : (jh + 1) * LIST_COLS]
+        def entries(lst, j0, j1):
+            return lst[:, j0 // PER_COLUMN : j1 // PER_COLUMN]
 
-        def byte_tile(name, width):
+        def plane(name, width):
             return keep.tile([P, width], U8, name=name, align_bytes=64)
 
-        tab2_sc = byte_tile("tab2_sc", T)
-        tab_sc = byte_tile("tab_sc", T)
-        wa_sc_raw = byte_tile("wa_sc_raw", H)
-        v_sc = [byte_tile("v_sc%d" % a, S) for a in range(PASSES)]
-        wa_sc = [byte_tile("wa_sc%d" % a, H) for a in range(PASSES)]
-        v2_sc = byte_tile("v2_sc", S)
+        tab2_sc, tab_sc, wa_sc_raw, v2_sc = plane("tab2_sc", T), plane("tab_sc", T), plane("wa_sc_raw", H), plane("v2_sc", S)
+        v_sc = [plane("v_sc%d" % a, S) for a in range(PASSES)]
+        wa_sc = [plane("wa_sc%d" % a, H) for a in range(PASSES)]
         nc.gpsimd.memset(tab2_sc[:].bitcast(I32), 0)
-        for plane in [tab_sc, wa_sc_raw] + v_sc[1:] + wa_sc[1:]:
-            nc.vector.memset(plane[:].bitcast(I32), 0)
+        for zeroed in [tab_sc, wa_sc_raw] + v_sc[1:] + wa_sc[1:]:
+            nc.vector.memset(zeroed[:].bitcast(I32), 0)
 
         warm = keep.tile([P, 2], F32, name="warm")
         nc.vector.memset(warm[:, 0:1], 1.0)
         nc.scalar.activation(warm[:, 1:2], warm[:, 0:1], ACT.Sqrt)
 
-        def load_scale_rows(engine, tile, scales):
-            passes = scales.shape[0]
-            for q in range(QUADS):
-                engine.dma_start(
-                    out=tile[32 * q : 32 * q + 4 * passes, :].bitcast(I32),
-                    in_=scales[:, 4 * q : 4 * q + 4, :].bitcast(I32),
+        def load_packed_planes(tile, scales):
+            for q in range(QUADRANTS):
+                nc.sync.dma_start(
+                    out=tile[32 * q : 32 * q + ROWS * PASSES, :].bitcast(I32),
+                    in_=scales[:, ROWS * q : ROWS * (q + 1), :].bitcast(I32),
                 )
-
-        def load_words(words, pool=windows, tag="window"):
-            w = pool.tile([P, T], I32, name=tag, align_bytes=64)
-            nc.sync.dma_start(out=w[:], in_=words.rearrange("p t i -> p (t i)").bitcast(I32))
-            return w
-
-        def load_weight(rows, pool=stage, tag="w_raw"):
-            raw = pool.tile([P, PACK, COLS], F32, name=tag)
-            nc.sync.dma_start(out=raw[:], in_=rows.rearrange("(p j) c -> p j c", j=PACK))
-            return raw
-
-        def round_weight(raw):
-            grouped = stage.tile([P, COLS * PACK], BF16, name="w_bf16", align_bytes=64)
-            nc.scalar.copy(
-                out=grouped[:].rearrange("p (t m j) -> p m j t", t=PACK, j=PACK),
-                in_=raw[:].rearrange("p j (m t) -> p m j t", t=PACK),
-            )
-            return grouped
-
-        def round_wo(raw):
-            grouped = stage.tile([P, COLS * PACK], BF16, name="w_bf16", align_bytes=64)
-            nc.scalar.copy(
-                out=grouped[:].rearrange("p (c i j) -> p c j i", i=4, j=PACK),
-                in_=raw[:].rearrange("p j (c i) -> p c j i", i=4),
-            )
-            return grouped
-
-        def quantize(name, grouped, tag=None):
-            width = grouped.shape[1] // PACK
-            codes = keep.tile([P, width], U32, name=tag or name + "_codes", align_bytes=64)
-            scales = byte_tile(name + "_scales", width)
-            nc.vector.quantize_mx(out=codes[:].bitcast(FP8X4), scales=scales[:], in_=grouped[:])
-            return codes, scales
-
-        def gather_words(name, window, lst):
-            halves = []
-            for jh in range(HALVES):
-                picked = keep.tile([P, COLS], U32, name="%s_%d" % (name, jh), align_bytes=64)
-                nc.vector.tensor_copy(picked[:], window[:].bitcast(U32).indirect(half_of(lst, jh)))
-                halves.append(picked)
-            return halves
 
         def shift_planes(planes):
             for a in range(1, PASSES):
                 nc.sync.dma_start(
                     out=planes[a][0:SHIFT_ROWS, :].bitcast(I32),
-                    in_=planes[0][4 * a : 4 * a + SHIFT_ROWS, :].bitcast(I32),
+                    in_=planes[0][ROWS * a : ROWS * a + SHIFT_ROWS, :].bitcast(I32),
                 )
 
-        wb_raw, wb_bf, wbq, tab_w, v, wo_raw, gates, wa_dealt = {}, {}, {}, {}, {}, {}, {}, {}
-        wa_raw = keep.tile([P, PASSES, H // 2], I32, name="wa_raw", align_bytes=64)
-        bias = keep.tile([P, PACK], F32, name="bias")
-        g_rows = gT.rearrange("(blk p t) c -> blk t p c", p=P, t=PACK)
+        def load_words(words):
+            window = windows.tile([P, T], I32, name="window", align_bytes=64)
+            nc.sync.dma_start(out=window[:], in_=words.rearrange("p t i -> p (t i)").bitcast(I32))
+            return window
 
-        def load_gate(blk, t):
-            g = windows.tile([P, T], F32, name="window", align_bytes=64)
-            nc.sync.dma_start(out=g[:], in_=g_rows[blk, t])
-            gates[blk, t] = g
+        def load_weight(rows, pool, tag):
+            raw = pool.tile([P, PACK, BANK], F32, name=tag)
+            nc.sync.dma_start(out=raw[:], in_=rows.rearrange("(p i) c -> p i c", i=PACK))
+            return raw
 
-        def deal(blk):
-            dealt = keep.tile([P, PASSES, 2 * KP], U8, name="wa_dealt%d" % blk, align_bytes=64)
-            nc.vector.tensor_copy(
-                out=dealt[:].bitcast(U16).rearrange("p a (t m) -> p a t m", t=PACK),
-                in_=wa_raw[:].bitcast(U16)[:, :, blk * KP : (blk + 1) * KP].rearrange("p a (m t) -> p a t m", t=PACK),
+        def gather_words(name, window, lst, j0, j1):
+            picked = keep.tile([P, j1 - j0], U32, name=name, align_bytes=64)
+            nc.vector.tensor_copy(picked[:], window[:].bitcast(U32).indirect(entries(lst, j0, j1)))
+            return picked
+
+        def round_and_deal(raw):
+            grouped = stage.tile([P, BANK * PACK], BF16, name="w_bf16", align_bytes=64)
+            nc.scalar.copy(
+                out=grouped[:].rearrange("p (t m i) -> p m i t", t=PACK, i=PACK),
+                in_=raw[:].rearrange("p i (m t) -> p m i t", t=PACK),
             )
-            wa_dealt[blk] = dealt
+            return grouped
 
-        wb_raw[0] = load_weight(wb[:, 0:COLS], keep, "slot0")
+        def round_and_interleave(copies, rows, pool, tag):
+            grouped = pool.tile([P, rows.shape[2] * PACK], BF16, name=tag, align_bytes=64)
+            share = rows.shape[2] // len(copies)
+            for c0, copy in zip(range(0, rows.shape[2], share), copies):
+                words = grouped[:, c0 * PACK : (c0 + share) * PACK]
+                copy(
+                    out=words.rearrange("p (c n i) -> p c i n", n=NEIGHBOURS, i=PACK),
+                    in_=rows[:, :, c0 : c0 + share].rearrange("p i (c n) -> p c i n", n=NEIGHBOURS),
+                )
+            return grouped
+
+        def quantize(name, grouped, codes_tag):
+            width = grouped.shape[1] // PACK
+            codes = keep.tile([P, width], U32, name=codes_tag, align_bytes=64)
+            scales = plane(name + "_scales", width)
+            nc.vector.quantize_mx(out=codes[:].bitcast(FP8X4), scales=scales[:], in_=grouped[:])
+            return codes, scales
+
         nc.sync.dma_start(list2[:], offs2)
         nc.sync.dma_start(list1[:], offs)
-        for r in range(4):
-            nc.sync.dma_start(out=tab2_sc[r:P:32, :].bitcast(I32), in_=tab2_scales[0, r:16:4, :].bitcast(I32))
+        wb_raw = [load_weight(wb[:, 0:KP], keep, "slot0")]
+        for s in range(ROWS):
+            nc.sync.dma_start(out=tab2_sc[s:P:32, :].bitcast(I32), in_=tab2_scales[0, s : QUADRANTS * ROWS : ROWS, :].bitcast(I32))
         tab2_w = load_words(tab2_words[0])
-        load_scale_rows(nc.sync, tab_sc, tab_scales)
-        wb_raw[1] = load_weight(wb[:, COLS : 2 * COLS], keep, "slot1")
-        tab_w[0] = load_words(tab_words[0])
-        load_scale_rows(nc.sync, wa_sc_raw, wa_scales)
+        load_packed_planes(tab_sc, tab_scales)
+        wb_raw.append(load_weight(wb[:, KP : 2 * KP], keep, "slot1"))
+        load_packed_planes(wa_sc_raw, wa_scales)
+        wa_raw = keep.tile([P, PASSES, H // 2], I32, name="wa_raw", align_bytes=64)
         nc.sync.dma_start(out=wa_raw[:], in_=wa_words.rearrange("a p e -> p a e").bitcast(I32))
-        tab_w[1] = load_words(tab_words[1])
+        tab_w = [load_words(tab_words[a]) for a in range(PASSES)]
+
         nc.vector.tensor_copy(v2_sc[:], tab2_sc[:].indirect(list2[:]))
-        v2 = gather_words("words", tab2_w, list2)
-        wb_bf[0] = round_weight(wb_raw[0])
-        wb_bf[1] = round_weight(wb_raw[1])
-        wbq[0] = quantize("wb0", wb_bf[0], "tab2_sc")
+        wb_bf = [round_and_deal(raw) for raw in wb_raw]
+        wbq = [quantize("wb0", wb_bf[0], "tab2_sc")]
+        v2 = gather_words("v2", tab2_w, list2, 0, S)
         nc.vector.tensor_copy(v_sc[0][:], tab_sc[:].indirect(list1[:]))
-        tab_w[2] = load_words(tab_words[2])
         shift_planes(v_sc)
-        v[0] = gather_words("v0", tab_w[0], list1)
         nc.vector.tensor_copy(
             out=wa_sc[0][:].rearrange("p (blk t m) -> p blk t m", blk=BLOCKS, t=PACK),
             in_=wa_sc_raw[:].rearrange("p (blk m t) -> p blk t m", blk=BLOCKS, t=PACK),
         )
         shift_planes(wa_sc)
-        wbq[1] = quantize("wb1", wb_bf[1], "wa_sc_raw")
-        deal(0)
-        v[1] = gather_words("v1", tab_w[1], list1)
-        v[2] = gather_words("v2", tab_w[2], list1)
-        deal(1)
-        load_gate(0, 0)
-        load_gate(0, 1)
-        load_gate(0, 2)
-        load_gate(0, 3)
-        wo_raw[0] = load_weight(wo[0:KP, :])
-        wo_raw[1] = load_weight(wo[KP : 2 * KP, :])
-        with nc.allow_non_contiguous_dma(reason="one bias value a partition and output tile"):
-            nc.sync.dma_start(out=bias[:], in_=b.rearrange("(c p) -> p c", p=P))
-        load_gate(1, 0)
-        load_gate(1, 1)
-        load_gate(1, 2)
-        load_gate(1, 3)
+        wa_dealt = keep.tile([P, PASSES, 2 * H], U8, name="wa_dealt", align_bytes=64)
+        nc.vector.tensor_copy(
+            out=wa_dealt[:].bitcast(U16).rearrange("p a (blk t m) -> p (a blk) t m", blk=BLOCKS, t=PACK),
+            in_=wa_raw[:].bitcast(U16).rearrange("p a (blk m t) -> p (a blk) t m", blk=BLOCKS, t=PACK),
+        )
+        wbq.append(quantize("wb1", wb_bf[1], "wa_raw"))
+        v = [gather_words("v_pass%d" % a, tab_w[a], list1, 0, S) for a in range(PASSES - 1)]
+        v_last = [gather_words("v_last%d" % j0, tab_w[2], list1, j0, j0 + BANK) for j0 in range(0, S, BANK)]
 
-        units = [(blk, jh, t) for blk in range(BLOCKS) for jh in range(HALVES) for t in range(PACK)]
-        groups = [(blk, jh) for blk in range(BLOCKS) for jh in range(HALVES)]
-        work = {}
-        for blk, jh, t in units:
-            if t == 0:
-                work[blk, jh] = keep.tile([P, PACK, COLS], F32, name="slot%d" % (groups.index((blk, jh)) + 1))
-            acc = psum.tile([P, COLS], F32, name="acc")
+        g_rows = gT.rearrange("(blk p t) c -> blk t p c", p=P, t=PACK)
+        bias = keep.tile([P, N // P], F32, name="bias")
+        saliency = {}
+        for blk in range(BLOCKS):
+            for t in range(PACK):
+                saliency[blk, t] = windows.tile([P, T], F32, name="window", align_bytes=64)
+                nc.sync.dma_start(out=saliency[blk, t][:], in_=g_rows[blk, t])
+            if blk == 0:
+                wo_raw = [load_weight(wo[r0 : r0 + KP, :], keep, "wo_raw%d" % r0) for r0 in range(0, H, KP)]
+                with nc.allow_non_contiguous_dma(reason="one bias value for each partition and tile of outputs"):
+                    nc.sync.dma_start(out=bias[:], in_=b.rearrange("(c p) -> p c", p=P))
+
+        parts = [(blk, j0) for blk in range(BLOCKS) for j0 in range(0, S, BANK)]
+        slots = ["slot%d" % n for n in range(len(parts) + 1)]
+        work = [keep.tile([P, PACK, BANK], F32, name=slot) for slot in slots[1:]]
+        slices = [(part, t) for part in range(len(parts)) for t in range(PACK)]
+
+        for part, t in slices:
+            blk, j0 = parts[part]
             codes, scales = wbq[blk]
+            q_bank = psum.tile([P, BANK], F32, name="ring_q")
             nc.tensor.matmul_mx(
-                out=acc[:],
+                out=q_bank[:],
                 lhsT=codes[:, t * P : (t + 1) * P].bitcast(FP8X4),
                 lhsT_scale=scales[:, t * P : (t + 1) * P],
-                rhs=v2[jh][:].bitcast(FP8X4),
-                rhs_scale=v2_sc[:, jh * COLS : (jh + 1) * COLS],
+                rhs=v2[:, j0 : j0 + BANK].bitcast(FP8X4),
+                rhs_scale=v2_sc[:, j0 : j0 + BANK],
                 start=True,
                 stop=True,
             )
-            nc.scalar.activation(work[blk, jh][:, t, :], acc[:], ACT.Copy)
+            nc.scalar.activation(work[part][:, t, :], q_bank[:], ACT.Copy)
 
-        def project(unit):
-            blk, jh, t = unit
-            acc = psum.tile([P, COLS], F32, name="fused")
+        def root(part, t):
+            blk, j0 = parts[part]
             col = blk * KP + t * P
+            p_bank = psum.tile([P, BANK], F32, name="ring_p")
+            moving = [picked[:, j0 : j0 + BANK] for picked in v] + [v_last[j0 // BANK][:]]
             for a in range(PASSES):
                 nc.tensor.matmul_mx(
-                    out=acc[:],
-                    lhsT=wa_dealt[blk][:, a, 2 * t * P : 2 * (t + 1) * P].bitcast(FP4X4),
+                    out=p_bank[:],
+                    lhsT=wa_dealt[:, a, 2 * col : 2 * (col + P)].bitcast(FP4X4),
                     lhsT_scale=wa_sc[a][:, col : col + P],
-                    rhs=v[a][jh][:].bitcast(FP8X4),
-                    rhs_scale=v_sc[a][:, jh * COLS : (jh + 1) * COLS],
+                    rhs=moving[a].bitcast(FP8X4),
+                    rhs_scale=v_sc[a][:, j0 : j0 + BANK],
                     start=(a == 0),
                     stop=(a == PASSES - 1),
                 )
-            w = work[blk, jh][:, t, :]
-            nc.vector.tensor_tensor(w, acc[:], w, ALU.mult)
-            nc.scalar.activation(w, w, ACT.Abs)
-            nc.scalar.activation(w, w, ACT.Sqrt)
+            values = work[part][:, t, :]
+            nc.vector.tensor_tensor(values, p_bank[:], values, ALU.mult)
+            nc.scalar.activation(values, values, ACT.Abs)
+            nc.scalar.activation(values, values, ACT.Sqrt)
 
-        pooled = {}
+        def gate(pooled, part, t, c0):
+            blk, j0 = parts[part]
+            c1 = c0 + pooled.shape[2]
+            picked = saliency[blk, t][:].indirect(entries(list1, j0 + c0, j0 + c1))
+            nc.vector.tensor_tensor(pooled[:, t, :], picked, work[part][:, t, c0:c1], ALU.mult)
 
-        def gate(group, c0, c1, slots=range(PACK)):
-            blk, jh = group
-            if group not in pooled:
-                pooled[group] = keep.tile([P, PACK, COLS], F32, name="slot%d" % groups.index(group))
-            first = (jh * COLS + c0) // 16
-            offsets = list1[:, first : first + (c1 - c0) // 16]
-            for t in slots:
-                nc.vector.tensor_tensor(
-                    pooled[group][:, t, c0:c1], gates[blk, t][:].indirect(offsets), work[group][:, t, c0:c1], ALU.mult
-                )
+        def open_banks(ring):
+            return [psum.tile([P, BANK], F32, name=ring) for c in range(N // P)]
 
-        def round_pooled(group, c0, c1, copy):
-            r = stage.tile([P, (c1 - c0) * PACK], BF16, name="pooled_bf16", align_bytes=64, bufs=3)
-            copy(
-                out=r[:].rearrange("p (c i t) -> p c t i", i=4, t=PACK),
-                in_=pooled[group][:, :, c0:c1].rearrange("p t (c i) -> p c t i", i=4),
-            )
-            return r
-
-        out_rows = out.rearrange("(c p) j -> p c j", p=P)
-
-        def fuse_pass(banks, blk, hq, c0, c1):
-            codes, scales = hq
-            for c in range(PACK):
+        def fuse(banks, blk, h_codes, c0, c1):
+            codes, scales = h_codes
+            for c, bank in enumerate(banks):
                 nc.tensor.matmul_mx(
-                    out=banks[c][:, 0 : c1 - c0],
+                    out=bank[:, 0 : c1 - c0],
                     lhsT=woq[blk][0][:, c * P : (c + 1) * P].bitcast(FP8X4),
                     lhsT_scale=woq[blk][1][:, c * P : (c + 1) * P],
                     rhs=codes[:, c0:c1].bitcast(FP8X4),
@@ -254,76 +224,53 @@ def tile_list_bilinear_region_word_kernel(
                     stop=(blk == BLOCKS - 1),
                 )
 
-        def store(banks, j0, width, share_with_vector):
-            for pair in range(PACK // 2):
-                y = results.tile([P, 2, width], F32, name="y_%d_%d" % (j0, pair))
-                for i in range(2):
-                    c = 2 * pair + i
-                    if share_with_vector and pair == 1:
-                        nc.vector.tensor_scalar(y[:, i, :], banks[c][:, 0:width], bias[:, c : c + 1], None, ALU.add)
+        out_rows = out.rearrange("(c p) j -> p c j", p=P)
+
+        def store(banks, j0, width, together, share):
+            for c0 in range(0, len(banks), together):
+                y = keep.tile([P, together, width], F32, name="y_%d_%d" % (j0, c0))
+                for c in range(c0, c0 + together):
+                    if share and 2 * c >= len(banks):
+                        nc.vector.tensor_scalar(y[:, c - c0, :], banks[c][:, 0:width], bias[:, c : c + 1], None, ALU.add)
                     else:
-                        nc.scalar.activation(y[:, i, :], banks[c][:, 0:width], ACT.Identity, bias=bias[:, c : c + 1])
-                nc.sync.dma_start(out=out_rows[:, 2 * pair : 2 * pair + 2, j0 : j0 + width], in_=y[:])
+                        nc.scalar.activation(y[:, c - c0, :], banks[c][:, 0:width], ACT.Identity, bias=bias[:, c : c + 1])
+                nc.sync.dma_start(out=out_rows[:, c0 : c0 + together, j0 : j0 + width], in_=y[:])
 
-        def open_banks(tag):
-            return [psum.tile([P, COLS], F32, name=tag) for c in range(PACK)]
+        last = len(parts) - 1
+        unrounded = {"wo0": wo_raw[0], "wo1": wo_raw[1]}
+        rounded, quantized = {}, {}
+        for step, (part, t) in enumerate(slices):
+            root(part, t)
+            if LAG <= step < last * PACK + LAG:
+                behind, t_behind = slices[step - LAG]
+                if t_behind == 0:
+                    unrounded["h%d" % behind] = keep.tile([P, PACK, BANK], F32, name=slots[behind])
+                gate(unrounded["h%d" % behind], behind, t_behind, 0)
+            for n, name in enumerate(["wo0", "h0", "wo1", "h1"]):
+                if step == FIRST_ROUND + 2 * (n + 1):
+                    quantized[name] = quantize(name, rounded[name], name + "_codes")
+                if step == FIRST_ROUND + 2 * n:
+                    rounded[name] = round_and_interleave([nc.scalar.copy], unrounded[name], stage, "w_bf16")
 
-        half = COLS // 2
-        last = groups[-1]
-        woq, wo_bf, hq, h_bf = {}, {}, {}, {}
-        project(units[0])
-        project(units[1])
-        project(units[2])
-        gate(units[0][:2], 0, COLS, [units[0][2]])
-        project(units[3])
-        gate(units[1][:2], 0, COLS, [units[1][2]])
-        project(units[4])
-        gate(units[2][:2], 0, COLS, [units[2][2]])
-        project(units[5])
-        gate(units[3][:2], 0, COLS, [units[3][2]])
-        project(units[6])
-        gate(units[4][:2], 0, COLS, [units[4][2]])
-        project(units[7])
-        gate(units[5][:2], 0, COLS, [units[5][2]])
-        wo_bf[0] = round_wo(wo_raw[0])
-        project(units[8])
-        gate(units[6][:2], 0, COLS, [units[6][2]])
-        project(units[9])
-        gate(units[7][:2], 0, COLS, [units[7][2]])
-        woq[0] = quantize("wo0", wo_bf[0])
-        h_bf[0, 0] = round_pooled((0, 0), 0, COLS, nc.scalar.copy)
-        project(units[10])
-        gate(units[8][:2], 0, COLS, [units[8][2]])
-        project(units[11])
-        gate(units[9][:2], 0, COLS, [units[9][2]])
-        hq[0, 0] = quantize("h00", h_bf[0, 0])
-        wo_bf[1] = round_wo(wo_raw[1])
-        project(units[12])
-        gate(units[10][:2], 0, COLS, [units[10][2]])
-        project(units[13])
-        woq[1] = quantize("wo1", wo_bf[1])
-        project(units[14])
-        project(units[15])
-        gate(units[11][:2], 0, COLS, [units[11][2]])
-        h_bf[1, 0] = round_pooled((1, 0), 0, COLS, nc.vector.tensor_copy)
-        h_bf[0, 1] = round_pooled((0, 1), 0, COLS, nc.scalar.copy)
-        banks_0 = open_banks("acc")
-        fuse_pass(banks_0, 0, hq[0, 0], 0, COLS)
-        gate(last, 0, half)
-        hq[1, 0] = quantize("h10", h_bf[1, 0])
-        hq[0, 1] = quantize("h01", h_bf[0, 1])
-        fuse_pass(banks_0, 1, hq[1, 0], 0, COLS)
-        banks_a = open_banks("fused")
-        fuse_pass(banks_a, 0, hq[0, 1], 0, half)
-        h_a = round_pooled(last, 0, half, nc.scalar.copy)
-        store(banks_0, 0, COLS, False)
-        hq_a = quantize("h11a", h_a)
-        banks_b = open_banks("acc")
-        fuse_pass(banks_b, 0, hq[0, 1], half, COLS)
-        gate(last, half, COLS)
-        fuse_pass(banks_a, 1, hq_a, 0, half)
-        store(banks_a, COLS, half, False)
-        h_b = round_pooled(last, half, COLS, nc.vector.tensor_copy)
-        hq_b = quantize("h11b", h_b)
-        fuse_pass(banks_b, 1, hq_b, 0, half)
-        store(banks_b, COLS + half, half, True)
+        woq = [quantized["wo0"], quantized["wo1"]]
+        banks_half, banks_a = open_banks("ring_q"), open_banks("ring_p")
+        fuse(banks_half, 0, quantized["h0"], 0, BANK)
+        fuse(banks_a, 0, quantized["h1"], 0, QUARTER)
+        h2_bf = round_and_interleave([nc.scalar.copy, nc.vector.tensor_copy], unrounded["h2"], keep, "h2_bf16")
+        h_a = keep.tile([P, PACK, QUARTER], F32, name=slots[last])
+        for t in range(PACK):
+            gate(h_a, last, t, 0)
+        fuse(banks_half, 1, quantize("h2", h2_bf, "h2_codes"), 0, BANK)
+        a_bf = round_and_interleave([nc.scalar.copy], h_a, stage, "w_bf16")
+        store(banks_half, 0, BANK, 1, False)
+        a_quantized = quantize("h_a", a_bf, "h_a_codes")
+        banks_b = open_banks("ring_q")
+        fuse(banks_b, 0, quantized["h1"], QUARTER, BANK)
+        h_b = keep.tile([P, PACK, QUARTER], F32, name="h2_bf16", align_bytes=64)
+        for t in range(PACK):
+            gate(h_b, last, t, QUARTER)
+        fuse(banks_a, 1, a_quantized, 0, QUARTER)
+        store(banks_a, BANK, QUARTER, 2, False)
+        b_bf = round_and_interleave([nc.vector.tensor_copy], h_b, stage, "w_bf16")
+        fuse(banks_b, 1, quantize("h_b", b_bf, "h_b_codes"), 0, QUARTER)
+        store(banks_b, BANK + QUARTER, QUARTER, 1, True)

from contextlib import ExitStack

import concourse.mybir as mybir

K, K2, T, S, H, N = 1536, 512, 2048, 1024, 1024, 512
FLOPS = 2 * S * (K * H + K2 * H + H * N)

F32 = mybir.dt.float32
BF16 = mybir.dt.bfloat16
I32 = mybir.dt.int32
U32 = mybir.dt.uint32
U16 = mybir.dt.uint16
U8 = mybir.dt.uint8
FP8X4 = mybir.dt.float8_e4m3fn_x4
FP4X4 = mybir.dt.float4_e2m1fn_x4
ACT = mybir.ActivationFunctionType
ALU = mybir.AluOpType

P = 128
PACK = 4
KP = P * PACK
PASSES = K // KP
BLOCKS = H // KP
BANK = 512
QUARTER = S // 4
PER_COLUMN = 16
QUADRANTS = 4
ROWS = 4
SHIFT_ROWS = 112
LAG = 2
FIRST_ROUND = 7
NEIGHBOURS = 4


def tile_list_bilinear_region_word_kernel(
    tc, tab_words, tab_scales, tab2_words, tab2_scales, offs, offs2, wa_words, wa_scales, wb, wo, gT, b, out
):
    nc = tc.nc
    with ExitStack() as ctx:
        keep = ctx.enter_context(tc.tile_pool(name="keep", bufs=1))
        windows = ctx.enter_context(tc.tile_pool(name="windows", bufs=10))
        stage = ctx.enter_context(tc.tile_pool(name="stage", bufs=3))
        psum = ctx.enter_context(tc.psum_pool(name="psum", bufs=4))

        list1 = keep.tile([P, S // PER_COLUMN], U16, name="list1")
        list2 = keep.tile([P, S // PER_COLUMN], U16, name="list2")

        def entries(lst, j0, j1):
            return lst[:, j0 // PER_COLUMN : j1 // PER_COLUMN]

        def plane(name, width):
            return keep.tile([P, width], U8, name=name, align_bytes=64)

        tab2_sc, tab_sc, wa_sc_raw, v2_sc = plane("tab2_sc", T), plane("tab_sc", T), plane("wa_sc_raw", H), plane("v2_sc", S)
        v_sc = [plane("v_sc%d" % a, S) for a in range(PASSES)]
        wa_sc = [plane("wa_sc%d" % a, H) for a in range(PASSES)]
        nc.gpsimd.memset(tab2_sc[:].bitcast(I32), 0)
        for zeroed in [tab_sc, wa_sc_raw] + v_sc[1:] + wa_sc[1:]:
            nc.vector.memset(zeroed[:].bitcast(I32), 0)

        warm = keep.tile([P, 2], F32, name="warm")
        nc.vector.memset(warm[:, 0:1], 1.0)
        nc.scalar.activation(warm[:, 1:2], warm[:, 0:1], ACT.Sqrt)

        def load_packed_planes(tile, scales):
            for q in range(QUADRANTS):
                nc.sync.dma_start(
                    out=tile[32 * q : 32 * q + ROWS * PASSES, :].bitcast(I32),
                    in_=scales[:, ROWS * q : ROWS * (q + 1), :].bitcast(I32),
                )

        def shift_planes(planes):
            for a in range(1, PASSES):
                nc.sync.dma_start(
                    out=planes[a][0:SHIFT_ROWS, :].bitcast(I32),
                    in_=planes[0][ROWS * a : ROWS * a + SHIFT_ROWS, :].bitcast(I32),
                )

        def load_words(words):
            window = windows.tile([P, T], I32, name="window", align_bytes=64)
            nc.sync.dma_start(out=window[:], in_=words.rearrange("p t i -> p (t i)").bitcast(I32))
            return window

        def load_weight(rows, pool, tag):
            raw = pool.tile([P, PACK, BANK], F32, name=tag)
            nc.sync.dma_start(out=raw[:], in_=rows.rearrange("(p i) c -> p i c", i=PACK))
            return raw

        def gather_words(name, window, lst, j0, j1):
            picked = keep.tile([P, j1 - j0], U32, name=name, align_bytes=64)
            nc.vector.tensor_copy(picked[:], window[:].bitcast(U32).indirect(entries(lst, j0, j1)))
            return picked

        def round_and_deal(raw):
            grouped = stage.tile([P, BANK * PACK], BF16, name="w_bf16", align_bytes=64)
            nc.scalar.copy(
                out=grouped[:].rearrange("p (t m i) -> p m i t", t=PACK, i=PACK),
                in_=raw[:].rearrange("p i (m t) -> p m i t", t=PACK),
            )
            return grouped

        def round_and_interleave(copies, rows, pool, tag):
            grouped = pool.tile([P, rows.shape[2] * PACK], BF16, name=tag, align_bytes=64)
            share = rows.shape[2] // len(copies)
            for c0, copy in zip(range(0, rows.shape[2], share), copies):
                words = grouped[:, c0 * PACK : (c0 + share) * PACK]
                copy(
                    out=words.rearrange("p (c n i) -> p c i n", n=NEIGHBOURS, i=PACK),
                    in_=rows[:, :, c0 : c0 + share].rearrange("p i (c n) -> p c i n", n=NEIGHBOURS),
                )
            return grouped

        def quantize(name, grouped, codes_tag):
            width = grouped.shape[1] // PACK
            codes = keep.tile([P, width], U32, name=codes_tag, align_bytes=64)
            scales = plane(name + "_scales", width)
            nc.vector.quantize_mx(out=codes[:].bitcast(FP8X4), scales=scales[:], in_=grouped[:])
            return codes, scales

        nc.sync.dma_start(list2[:], offs2)
        nc.sync.dma_start(list1[:], offs)
        wb_raw = [load_weight(wb[:, 0:KP], keep, "slot0")]
        for s in range(ROWS):
            nc.sync.dma_start(out=tab2_sc[s:P:32, :].bitcast(I32), in_=tab2_scales[0, s : QUADRANTS * ROWS : ROWS, :].bitcast(I32))
        tab2_w = load_words(tab2_words[0])
        load_packed_planes(tab_sc, tab_scales)
        wb_raw.append(load_weight(wb[:, KP : 2 * KP], keep, "slot1"))
        load_packed_planes(wa_sc_raw, wa_scales)
        wa_raw = keep.tile([P, PASSES, H // 2], I32, name="wa_raw", align_bytes=64)
        nc.sync.dma_start(out=wa_raw[:], in_=wa_words.rearrange("a p e -> p a e").bitcast(I32))
        tab_w = [load_words(tab_words[a]) for a in range(PASSES)]

        nc.vector.tensor_copy(v2_sc[:], tab2_sc[:].indirect(list2[:]))
        wb_bf = [round_and_deal(raw) for raw in wb_raw]
        wbq = [quantize("wb0", wb_bf[0], "tab2_sc")]
        v2 = gather_words("v2", tab2_w, list2, 0, S)
        nc.vector.tensor_copy(v_sc[0][:], tab_sc[:].indirect(list1[:]))
        shift_planes(v_sc)
        nc.vector.tensor_copy(
            out=wa_sc[0][:].rearrange("p (blk t m) -> p blk t m", blk=BLOCKS, t=PACK),
            in_=wa_sc_raw[:].rearrange("p (blk m t) -> p blk t m", blk=BLOCKS, t=PACK),
        )
        shift_planes(wa_sc)
        wa_dealt = keep.tile([P, PASSES, 2 * H], U8, name="wa_dealt", align_bytes=64)
        nc.vector.tensor_copy(
            out=wa_dealt[:].bitcast(U16).rearrange("p a (blk t m) -> p (a blk) t m", blk=BLOCKS, t=PACK),
            in_=wa_raw[:].bitcast(U16).rearrange("p a (blk m t) -> p (a blk) t m", blk=BLOCKS, t=PACK),
        )
        wbq.append(quantize("wb1", wb_bf[1], "wa_raw"))
        v = [gather_words("v_pass%d" % a, tab_w[a], list1, 0, S) for a in range(PASSES - 1)]
        v_last = [gather_words("v_last%d" % j0, tab_w[2], list1, j0, j0 + BANK) for j0 in range(0, S, BANK)]

        g_rows = gT.rearrange("(blk p t) c -> blk t p c", p=P, t=PACK)
        bias = keep.tile([P, N // P], F32, name="bias")
        saliency = {}
        for blk in range(BLOCKS):
            for t in range(PACK):
                saliency[blk, t] = windows.tile([P, T], F32, name="window", align_bytes=64)
                nc.sync.dma_start(out=saliency[blk, t][:], in_=g_rows[blk, t])
            if blk == 0:
                wo_raw = [load_weight(wo[r0 : r0 + KP, :], keep, "wo_raw%d" % r0) for r0 in range(0, H, KP)]
                with nc.allow_non_contiguous_dma(reason="one bias value for each partition and tile of outputs"):
                    nc.sync.dma_start(out=bias[:], in_=b.rearrange("(c p) -> p c", p=P))

        parts = [(blk, j0) for blk in range(BLOCKS) for j0 in range(0, S, BANK)]
        slots = ["slot%d" % n for n in range(len(parts) + 1)]
        work = [keep.tile([P, PACK, BANK], F32, name=slot) for slot in slots[1:]]
        slices = [(part, t) for part in range(len(parts)) for t in range(PACK)]

        for part, t in slices:
            blk, j0 = parts[part]
            codes, scales = wbq[blk]
            q_bank = psum.tile([P, BANK], F32, name="ring_q")
            nc.tensor.matmul_mx(
                out=q_bank[:],
                lhsT=codes[:, t * P : (t + 1) * P].bitcast(FP8X4),
                lhsT_scale=scales[:, t * P : (t + 1) * P],
                rhs=v2[:, j0 : j0 + BANK].bitcast(FP8X4),
                rhs_scale=v2_sc[:, j0 : j0 + BANK],
                start=True,
                stop=True,
            )
            nc.scalar.activation(work[part][:, t, :], q_bank[:], ACT.Copy)

        def root(part, t):
            blk, j0 = parts[part]
            col = blk * KP + t * P
            p_bank = psum.tile([P, BANK], F32, name="ring_p")
            moving = [picked[:, j0 : j0 + BANK] for picked in v] + [v_last[j0 // BANK][:]]
            for a in range(PASSES):
                nc.tensor.matmul_mx(
                    out=p_bank[:],
                    lhsT=wa_dealt[:, a, 2 * col : 2 * (col + P)].bitcast(FP4X4),
                    lhsT_scale=wa_sc[a][:, col : col + P],
                    rhs=moving[a].bitcast(FP8X4),
                    rhs_scale=v_sc[a][:, j0 : j0 + BANK],
                    start=(a == 0),
                    stop=(a == PASSES - 1),
                )
            values = work[part][:, t, :]
            nc.vector.tensor_tensor(values, p_bank[:], values, ALU.mult)
            nc.scalar.activation(values, values, ACT.Abs)
            nc.scalar.activation(values, values, ACT.Sqrt)

        def gate(pooled, part, t, c0):
            blk, j0 = parts[part]
            c1 = c0 + pooled.shape[2]
            picked = saliency[blk, t][:].indirect(entries(list1, j0 + c0, j0 + c1))
            nc.vector.tensor_tensor(pooled[:, t, :], picked, work[part][:, t, c0:c1], ALU.mult)

        def open_banks(ring):
            return [psum.tile([P, BANK], F32, name=ring) for c in range(N // P)]

        def fuse(banks, blk, h_codes, c0, c1):
            codes, scales = h_codes
            for c, bank in enumerate(banks):
                nc.tensor.matmul_mx(
                    out=bank[:, 0 : c1 - c0],
                    lhsT=woq[blk][0][:, c * P : (c + 1) * P].bitcast(FP8X4),
                    lhsT_scale=woq[blk][1][:, c * P : (c + 1) * P],
                    rhs=codes[:, c0:c1].bitcast(FP8X4),
                    rhs_scale=scales[:, c0:c1],
                    start=(blk == 0),
                    stop=(blk == BLOCKS - 1),
                )

        out_rows = out.rearrange("(c p) j -> p c j", p=P)

        def store(banks, j0, width, together, share):
            for c0 in range(0, len(banks), together):
                y = keep.tile([P, together, width], F32, name="y_%d_%d" % (j0, c0))
                for c in range(c0, c0 + together):
                    if share and 2 * c >= len(banks):
                        nc.vector.tensor_scalar(y[:, c - c0, :], banks[c][:, 0:width], bias[:, c : c + 1], None, ALU.add)
                    else:
                        nc.scalar.activation(y[:, c - c0, :], banks[c][:, 0:width], ACT.Identity, bias=bias[:, c : c + 1])
                nc.sync.dma_start(out=out_rows[:, c0 : c0 + together, j0 : j0 + width], in_=y[:])

        last = len(parts) - 1
        unrounded = {"wo0": wo_raw[0], "wo1": wo_raw[1]}
        rounded, quantized = {}, {}
        for step, (part, t) in enumerate(slices):
            root(part, t)
            if LAG <= step < last * PACK + LAG:
                behind, t_behind = slices[step - LAG]
                if t_behind == 0:
                    unrounded["h%d" % behind] = keep.tile([P, PACK, BANK], F32, name=slots[behind])
                gate(unrounded["h%d" % behind], behind, t_behind, 0)
            for n, name in enumerate(["wo0", "h0", "wo1", "h1"]):
                if step == FIRST_ROUND + 2 * (n + 1):
                    quantized[name] = quantize(name, rounded[name], name + "_codes")
                if step == FIRST_ROUND + 2 * n:
                    rounded[name] = round_and_interleave([nc.scalar.copy], unrounded[name], stage, "w_bf16")

        woq = [quantized["wo0"], quantized["wo1"]]
        banks_half, banks_a = open_banks("ring_q"), open_banks("ring_p")
        fuse(banks_half, 0, quantized["h0"], 0, BANK)
        fuse(banks_a, 0, quantized["h1"], 0, QUARTER)
        h2_bf = round_and_interleave([nc.scalar.copy, nc.vector.tensor_copy], unrounded["h2"], keep, "h2_bf16")
        h_a = keep.tile([P, PACK, QUARTER], F32, name=slots[last])
        for t in range(PACK):
            gate(h_a, last, t, 0)
        fuse(banks_half, 1, quantize("h2", h2_bf, "h2_codes"), 0, BANK)
        a_bf = round_and_interleave([nc.scalar.copy], h_a, stage, "w_bf16")
        store(banks_half, 0, BANK, 1, False)
        a_quantized = quantize("h_a", a_bf, "h_a_codes")
        banks_b = open_banks("ring_q")
        fuse(banks_b, 0, quantized["h1"], QUARTER, BANK)
        h_b = keep.tile([P, PACK, QUARTER], F32, name="h2_bf16", align_bytes=64)
        for t in range(PACK):
            gate(h_b, last, t, QUARTER)
        fuse(banks_a, 1, a_quantized, 0, QUARTER)
        store(banks_a, BANK, QUARTER, 2, False)
        b_bf = round_and_interleave([nc.vector.tensor_copy], h_b, stage, "w_bf16")
        fuse(banks_b, 1, quantize("h_b", b_bf, "h_b_codes"), 0, QUARTER)
        store(banks_b, BANK + QUARTER, QUARTER, 1, True)
